import numpy as np
import ml_dtypes


def mxq(x, axis, fmt="e4m3"):
    dtype, down = {"e4m3": (ml_dtypes.float8_e4m3fn, 7), "e5m2": (ml_dtypes.float8_e5m2, 14)}[fmt]
    v = np.moveaxis(np.asarray(x, np.float32).astype(ml_dtypes.bfloat16).astype(np.float64), axis, -1)
    blocks = v.reshape(v.shape[:-1] + (-1, 32))
    amax = np.abs(blocks).max(-1, keepdims=True)
    byte = np.maximum(np.where(amax > 0, np.frexp(amax)[1] - 1 + 127, 0) - down, 1)
    scale = np.exp2(byte - 127.0)
    codes = (blocks / scale).astype(np.float32).astype(dtype).astype(np.float64)
    return np.moveaxis((codes * scale).reshape(v.shape), -1, axis)


WIDE = False


def mx_kscale(k):
    if not WIDE:
        return np.ones(k)
    levels = np.array([10, -10, 5, -5, 0])
    if k % 512:
        return np.exp2(np.random.permutation(np.resize(levels, k // 32))).repeat(32)
    a = np.empty((k // 512, 16))
    for p in range(k // 512):
        a[p, :8] = np.random.permutation(np.resize(levels, 8))
        for g in range(8):
            far = levels[np.abs(levels - a[p, g]) >= 10]
            a[p, g + 8] = far[np.random.randint(len(far))]
    return np.exp2(a.ravel()).repeat(32)


def f64(x):
    return np.asarray(x).astype(np.float64)


def striped(idx):
    return np.tile(idx.reshape(-1, 16).T, (8, 1)).astype(np.uint16)


def unstriped(offs):
    return offs[:16].T.reshape(-1).astype(np.int64)


def sigmoid(v):
    return 1.0 / (1.0 + np.exp(-np.maximum(v, -700.0)))


K, T, S, H, N = 1024, 2048, 1024, 512, 512


def setup_inputs():
    n = np.random.standard_normal
    s = mx_kscale(K)[:, None]
    u = mx_kscale(H)
    return {
        "xT": (n((K, T)) * s).astype(np.float32),
        "w1": (n((K, H)) / np.sqrt(K) / s).astype(np.float32),
        "w3": (n((K, H)) / np.sqrt(K) / s * u).astype(np.float32),
        "w2": (n((H, N)) / np.sqrt(H) / u[:, None]).astype(np.float32),
        "offs": striped(np.sort(np.random.permutation(T)[:S])),
    }


def reference(xT, w1, w3, w2, offs):
    idx = unstriped(offs)
    xq = mxq(f64(xT)[:, idx], 0, "e4m3")
    h = sigmoid(mxq(f64(w1), 0, "e4m3").T @ xq) * (mxq(f64(w3), 0, "e4m3").T @ xq)
    y = mxq(f64(w2), 0, "e4m3").T @ mxq(h, 0, "e4m3")
    return y

@@ -1,0 +1,251 @@
+from contextlib import ExitStack
+
+import concourse.mybir as mybir
+
+K, T, S, H, N = 1024, 2048, 1024, 512, 512
+FLOPS = 2 * S * (2 * K * H + H * N)
+
+F32 = mybir.dt.float32
+BF16 = mybir.dt.bfloat16
+U32 = mybir.dt.uint32
+U16 = mybir.dt.uint16
+U8 = mybir.dt.uint8
+FP8X4 = mybir.dt.float8_e4m3fn_x4
+SIGMOID = mybir.ActivationFunctionType.Sigmoid
+MULT = mybir.AluOpType.mult
+
+P = 128
+PACK = 4
+K_PASS = P * PACK
+PASSES = K // K_PASS
+X_LOADS = (
+    ((0, 512), (512, 512), (1024, 512), (1536, 512)),
+    ((0, 512), (512, 512), (1024, 512), (1536, 512)),
+)
+HALF = 512
+STRIP = 128
+STRIPS = S // STRIP
+PAIR = 2 * STRIP
+
+
+def tile_picked_pick_glu_sigmoid_srt_e_kernel(tc, xT, w1, w3, w2, offs, out):
+    nc = tc.nc
+
+    with ExitStack() as ctx:
+        lists = ctx.enter_context(tc.tile_pool(name="lists", bufs=1))
+        keep = ctx.enter_context(tc.tile_pool(name="keep", bufs=1))
+        ring = ctx.enter_context(tc.tile_pool(name="ring", bufs=4))
+        psum = ctx.enter_context(tc.psum_pool(name="psum", bufs=8))
+
+        offsets = lists.tile([P, S // 16], U16, name="offsets")
+
+        x_codes = [keep.tile([P, T], U32, name=f"x_codes{s}", align_bytes=64) for s in range(PASSES)]
+        x_scales = [keep.tile([P, T], U8, name=f"x_scales{s}", align_bytes=64) for s in range(PASSES)]
+        g_codes = [keep.tile([P, S], U32, name=f"g_codes{s}", align_bytes=64) for s in range(PASSES)]
+        g_scales = [keep.tile([P, S], U8, name=f"g_scales{s}", align_bytes=64) for s in range(PASSES)]
+
+        warm_in = keep.tile([P, 1], F32, name="warm_in")
+        warm_out = keep.tile([P, 1], F32, name="warm_out")
+        nc.gpsimd.memset(warm_in[:], 0.0)
+        nc.scalar.activation(warm_out[:], warm_in[:], SIGMOID)
+        for s in range(PASSES):
+            nc.gpsimd.memset(x_scales[s][:], 0)
+
+        def weight(name, src):
+            raw = keep.tile([P, PACK, 512], F32, name=f"{name}_raw")
+            return (
+                src.rearrange("(p j) c -> p j c", j=PACK),
+                raw,
+                keep.tile([P, 512], U32, name=f"{name}_codes", align_bytes=64),
+                keep.tile([P, 512], U8, name=f"{name}_scales", align_bytes=64),
+            )
+
+        units = {}
+        for s in range(PASSES):
+            for q, (first, width) in enumerate(X_LOADS[s]):
+                cols = slice(first, first + width)
+                raw = keep.tile([P, PACK, width], F32, name=f"x_raw{s}_{q}")
+                src = xT[s * K_PASS : (s + 1) * K_PASS, cols].rearrange("(p j) c -> p j c", j=PACK)
+                units["x", s, q] = (src, raw, x_codes[s][:, cols], x_scales[s][:, cols], False)
+        w_codes = {}
+        for name, src, permute in (
+            ("w1_0", w1[0:K_PASS, :], True),
+            ("w1_1", w1[K_PASS:K, :], True),
+            ("w3_0", w3[0:K_PASS, :], True),
+            ("w3_1", w3[K_PASS:K, :], True),
+            ("w2", w2, False),
+        ):
+            view, raw, codes, scales = weight(name, src)
+            w_codes[name] = (codes, scales)
+            units[name] = (view, raw, codes[:], scales[:], permute)
+
+        for u, unit in units.items():
+            if u == "w3_1":
+                for a in (0, 256):
+                    nc.sync.dma_start(out=unit[1][:, :, a : a + 256], in_=unit[0][:, :, a : a + 256])
+            else:
+                nc.sync.dma_start(out=unit[1][:], in_=unit[0])
+            if u == ("x", 0, 1):
+                nc.sync.dma_start(offsets[:], offs)
+
+        grouped = {}
+
+        def interleave(u, engine, a, b):
+            src, raw, codes, scales, permute = units[u]
+            width = raw.shape[2]
+            if u not in grouped:
+                grouped[u] = ring.tile([P, width * PACK], BF16, name="grouped", align_bytes=64)
+            i = raw[:, :, a:b].rearrange("p j (c i) -> p c j i", i=4)
+            if permute:
+                o = grouped[u][:].rearrange("p (t m j) -> p m j t", t=4, j=PACK)[:, a // 4 : b // 4, :, :]
+            else:
+                o = grouped[u][:].rearrange("p (c i j) -> p c j i", i=4, j=PACK)[:, a // 4 : b // 4, :, :]
+            if engine == "scalar":
+                nc.scalar.copy(o, i)
+            else:
+                nc.vector.tensor_copy(o, i)
+
+        def quantise(u):
+            nc.vector.quantize_mx(out=units[u][2].bitcast(FP8X4), scales=units[u][3], in_=grouped[u][:])
+
+        def gather(table, picked, a=0, b=S):
+            nc.vector.tensor_copy(picked[:, a:b], table[:].indirect(offsets[:, a // 16 : b // 16]))
+
+        for s in range(PASSES):
+            for q, (first, width) in enumerate(X_LOADS[s]):
+                u = ("x", s, q)
+                share = 336 if width == 512 else 96
+                interleave(u, "scalar", 0, share)
+                interleave(u, "vector", share, width)
+                quantise(u)
+                if (s, q) == (1, 0):
+                    gather(x_codes[0], g_codes[0])
+                if (s, q) == (1, 1):
+                    gather(x_scales[0], g_scales[0])
+        gather(x_scales[1], g_scales[1])
+        gather(x_codes[1], g_codes[1], 0, HALF)
+        interleave("w1_0", "scalar", 0, 448)
+        interleave("w1_0", "vector", 448, 512)
+        quantise("w1_0")
+        gather(x_codes[1], g_codes[1], HALF, S)
+        interleave("w1_1", "scalar", 0, 448)
+        interleave("w1_1", "vector", 448, 512)
+        quantise("w1_1")
+
+        def product(acc, name, t, s, cols, start, stop):
+            codes, scales = w_codes[name]
+            rows = slice(t * P, (t + 1) * P)
+            nc.tensor.matmul_mx(
+                out=acc,
+                lhsT=codes[:, rows].bitcast(FP8X4),
+                lhsT_scale=scales[:, rows],
+                rhs=g_codes[s][:, cols].bitcast(FP8X4),
+                rhs_scale=g_scales[s][:, cols],
+                start=start,
+                stop=stop,
+            )
+
+        warm = psum.tile([P, HALF], F32, name="bank")
+        for e in range(4):
+            nc.tensor.matmul_mx(
+                out=warm[:],
+                lhsT=g_codes[1][:, 0:P].bitcast(FP8X4),
+                lhsT_scale=g_scales[1][:, 0:P],
+                rhs=g_codes[1][:, 0:HALF].bitcast(FP8X4),
+                rhs_scale=g_scales[1][:, 0:HALF],
+                start=True,
+                stop=True,
+            )
+        banks = {}
+        gates = []
+        for half in range(2):
+            gates.append(keep.tile([P, PACK, HALF], F32, name=f"gate{half}"))
+            for t in range(PACK):
+                banks[half, t] = psum.tile([P, HALF], F32, name="bank")
+        for s in range(PASSES):
+            for half in range(2):
+                for t in range(PACK):
+                    product(banks[half, t][:], f"w1_{s}", t, s, slice(half * HALF, (half + 1) * HALF), s == 0, s == 1)
+        interleave("w3_0", "scalar", 0, 256)
+        interleave("w3_0", "vector", 256, 512)
+        quantise("w3_0")
+        interleave("w3_1", "scalar", 0, 256)
+        interleave("w3_1", "scalar", 256, 352)
+        interleave("w3_1", "vector", 352, 512)
+        quantise("w3_1")
+        for half in range(2):
+            for t in range(PACK):
+                nc.scalar.activation(gates[half][:, t, :], banks[half, t][:], SIGMOID)
+
+        h_grouped = keep.tile([P, S * PACK], BF16, name="h_grouped", align_bytes=64)
+        h_codes = keep.tile([P, S], U32, name="h_codes", align_bytes=64)
+        h_scales = keep.tile([P, S], U8, name="h_scales", align_bytes=64)
+        out_rows = out.rearrange("(b p) n -> p b n", p=P)
+
+        def second(first, width, engines):
+            cols = slice(first, first + width)
+            codes, scales = w_codes["w2"]
+            y = keep.tile([P, N // P, width], F32, name=f"y{first}")
+            per_bank = HALF // width
+            for g in range(N // P // per_bank):
+                acc = psum.tile([P, per_bank, width], F32, name="bank")
+                for e in range(per_bank):
+                    b = per_bank * g + e
+                    rows = slice(b * P, (b + 1) * P)
+                    nc.tensor.matmul_mx(
+                        out=acc[:, e, :],
+                        lhsT=codes[:, rows].bitcast(FP8X4),
+                        lhsT_scale=scales[:, rows],
+                        rhs=h_codes[:, cols].bitcast(FP8X4),
+                        rhs_scale=h_scales[:, cols],
+                        start=True,
+                        stop=True,
+                    )
+                group = y[:, per_bank * g : per_bank * (g + 1), :]
+                if engines[g] == "S":
+                    nc.scalar.copy(group, acc[:])
+                else:
+                    nc.vector.tensor_copy(group, acc[:])
+                nc.sync.dma_start(out=out_rows[:, per_bank * g : per_bank * (g + 1), cols], in_=group)
+
+        def gated(c):
+            acc = strips[c]
+            half, first = divmod(c * STRIP, HALF)
+            nc.vector.tensor_tensor(
+                out=h_grouped[:, c * STRIP * PACK : (c + 1) * STRIP * PACK].rearrange("p (c i t) -> p c t i", i=4, t=PACK),
+                in0=acc[:].rearrange("p t (c i) -> p c t i", i=4),
+                in1=gates[half][:, :, first : first + STRIP].rearrange("p t (c i) -> p c t i", i=4),
+                op=MULT,
+            )
+
+        def quantise_h(c, n):
+            cols = slice(c * STRIP, (c + n) * STRIP)
+            nc.vector.quantize_mx(
+                out=h_codes[:, cols].bitcast(FP8X4),
+                scales=h_scales[:, cols],
+                in_=h_grouped[:, c * STRIP * PACK : (c + n) * STRIP * PACK],
+            )
+
+        strips = {}
+        for c in range(STRIPS):
+            strips[c] = psum.tile([P, PACK, STRIP], F32, name="bank")
+            for t in range(PACK):
+                for s in range(PASSES):
+                    product(strips[c][:, t, :], f"w3_{s}", t, s, slice(c * STRIP, (c + 1) * STRIP), s == 0, s == 1)
+            gated(c)
+            if c == 2:
+                quantise_h(0, 2)
+                interleave("w2", "vector", 0, 512)
+                quantise("w2")
+            if c == 4:
+                quantise_h(2, 2)
+                second(0, 256, "SS")
+            if c == 6:
+                quantise_h(4, 2)
+                second(256, 256, "SS")
+            if c == 7:
+                second(512, 256, "SS")
+                quantise_h(6, 1)
+                second(768, 128, "S")
+                quantise_h(7, 1)
+                second(896, 128, "V")

@@ -18,14 +18,10 @@ P = 128
 PACK = 4
 K_PASS = P * PACK
 PASSES = K // K_PASS
-X_LOADS = (
-    ((0, 512), (512, 512), (1024, 512), (1536, 512)),
-    ((0, 512), (512, 512), (1024, 512), (1536, 512)),
-)
 HALF = 512
 STRIP = 128
 STRIPS = S // STRIP
-PAIR = 2 * STRIP
+PACKED = True
 
 
 def tile_picked_pick_glu_sigmoid_srt_e_kernel(tc, xT, w1, w3, w2, offs, out):
@@ -34,186 +30,121 @@ def tile_picked_pick_glu_sigmoid_srt_e_kernel(tc, xT, w1, w3, w2, offs, out):
     with ExitStack() as ctx:
         lists = ctx.enter_context(tc.tile_pool(name="lists", bufs=1))
         keep = ctx.enter_context(tc.tile_pool(name="keep", bufs=1))
-        ring = ctx.enter_context(tc.tile_pool(name="ring", bufs=4))
+        ring = ctx.enter_context(tc.tile_pool(name="ring", bufs=5))
         psum = ctx.enter_context(tc.psum_pool(name="psum", bufs=8))
 
         offsets = lists.tile([P, S // 16], U16, name="offsets")
 
         x_codes = [keep.tile([P, T], U32, name=f"x_codes{s}", align_bytes=64) for s in range(PASSES)]
-        x_scales = [keep.tile([P, T], U8, name=f"x_scales{s}", align_bytes=64) for s in range(PASSES)]
         g_codes = [keep.tile([P, S], U32, name=f"g_codes{s}", align_bytes=64) for s in range(PASSES)]
-        g_scales = [keep.tile([P, S], U8, name=f"g_scales{s}", align_bytes=64) for s in range(PASSES)]
+        if PACKED:
+            x_plane = keep.tile([P, T], U8, name="x_plane", align_bytes=64)
+            g_plane = keep.tile([P, S], U8, name="g_plane", align_bytes=64)
+            x_scales = [x_plane, x_plane]
+            g_scales = [g_plane, g_plane]
+        else:
+            x_scales = [keep.tile([P, T], U8, name=f"x_scales{s}", align_bytes=64) for s in range(PASSES)]
+            g_scales = [keep.tile([P, S], U8, name=f"g_scales{s}", align_bytes=64) for s in range(PASSES)]
+        row0 = (0, 4) if PACKED else (0, 0)
 
         warm_in = keep.tile([P, 1], F32, name="warm_in")
         warm_out = keep.tile([P, 1], F32, name="warm_out")
         nc.gpsimd.memset(warm_in[:], 0.0)
         nc.scalar.activation(warm_out[:], warm_in[:], SIGMOID)
-        for s in range(PASSES):
-            nc.gpsimd.memset(x_scales[s][:], 0)
+        for plane in x_scales[:1] if PACKED else x_scales:
+            nc.gpsimd.memset(plane[:], 0)
 
-        def weight(name, src):
-            raw = keep.tile([P, PACK, 512], F32, name=f"{name}_raw")
-            return (
-                src.rearrange("(p j) c -> p j c", j=PACK),
-                raw,
-                keep.tile([P, 512], U32, name=f"{name}_codes", align_bytes=64),
-                keep.tile([P, 512], U8, name=f"{name}_scales", align_bytes=64),
-            )
+        w_src = {"w1_0": w1[0:K_PASS, :], "w1_1": w1[K_PASS:K, :], "w3_0": w3[0:K_PASS, :], "w3_1": w3[K_PASS:K, :], "w2": w2}
+        w_raw = {u: keep.tile([P, PACK, 512], F32, name=f"{u}_raw") for u in w_src}
+        w_codes = {u: keep.tile([P, 512], U32, name=f"{u}_codes", align_bytes=64) for u in w_src}
+        w_scales = {u: keep.tile([P, 512], U8, name=f"{u}_scales", align_bytes=64) for u in w_src}
+        x_raw = {}
 
-        units = {}
-        for s in range(PASSES):
-            for q, (first, width) in enumerate(X_LOADS[s]):
-                cols = slice(first, first + width)
-                raw = keep.tile([P, PACK, width], F32, name=f"x_raw{s}_{q}")
-                src = xT[s * K_PASS : (s + 1) * K_PASS, cols].rearrange("(p j) c -> p j c", j=PACK)
-                units["x", s, q] = (src, raw, x_codes[s][:, cols], x_scales[s][:, cols], False)
-        w_codes = {}
-        for name, src, permute in (
-            ("w1_0", w1[0:K_PASS, :], True),
-            ("w1_1", w1[K_PASS:K, :], True),
-            ("w3_0", w3[0:K_PASS, :], True),
-            ("w3_1", w3[K_PASS:K, :], True),
-            ("w2", w2, False),
-        ):
-            view, raw, codes, scales = weight(name, src)
-            w_codes[name] = (codes, scales)
-            units[name] = (view, raw, codes[:], scales[:], permute)
+        def load_x(s, j, first, width):
+            x_raw[s, j] = keep.tile([P, PACK, width], F32, name=f"x_raw{s}_{j}")
+            src = xT[s * K_PASS : (s + 1) * K_PASS, first : first + width]
+            nc.sync.dma_start(out=x_raw[s, j][:], in_=src.rearrange("(p j) c -> p j c", j=PACK))
 
-        for u, unit in units.items():
-            if u == "w3_1":
-                for a in (0, 256):
-                    nc.sync.dma_start(out=unit[1][:, :, a : a + 256], in_=unit[0][:, :, a : a + 256])
-            else:
-                nc.sync.dma_start(out=unit[1][:], in_=unit[0])
-            if u == ("x", 0, 1):
-                nc.sync.dma_start(offsets[:], offs)
+        def load_w(u, a, b):
+            nc.sync.dma_start(out=w_raw[u][:, :, a:b], in_=w_src[u].rearrange("(p j) c -> p j c", j=PACK)[:, :, a:b])
 
         grouped = {}
 
-        def interleave(u, engine, a, b):
-            src, raw, codes, scales, permute = units[u]
-            width = raw.shape[2]
+        def interleave(u, copy, a, b):
             if u not in grouped:
-                grouped[u] = ring.tile([P, width * PACK], BF16, name="grouped", align_bytes=64)
-            i = raw[:, :, a:b].rearrange("p j (c i) -> p c j i", i=4)
-            if permute:
-                o = grouped[u][:].rearrange("p (t m j) -> p m j t", t=4, j=PACK)[:, a // 4 : b // 4, :, :]
+                grouped[u] = ring.tile([P, 512 * PACK], BF16, name="grouped", align_bytes=64)
+            if u[0] == "x":
+                raw = x_raw[u[1], u[2]][:, :, u[3] + a : u[3] + b]
             else:
+                raw = w_raw[u][:, :, a:b]
+            i = raw.rearrange("p j (c i) -> p c j i", i=4)
+            if u[0] == "x" or u == "w2":
                 o = grouped[u][:].rearrange("p (c i j) -> p c j i", i=4, j=PACK)[:, a // 4 : b // 4, :, :]
-            if engine == "scalar":
-                nc.scalar.copy(o, i)
             else:
-                nc.vector.tensor_copy(o, i)
+                o = grouped[u][:].rearrange("p (t m j) -> p m j t", t=4, j=PACK)[:, a // 4 : b // 4, :, :]
+            copy(o, i)
 
         def quantise(u):
-            nc.vector.quantize_mx(out=units[u][2].bitcast(FP8X4), scales=units[u][3], in_=grouped[u][:])
+            if u[0] == "x":
+                s, width, first = u[1], u[4], u[5]
+                codes, scales = x_codes[s][:, first : first + width], x_scales[s][row0[s] :, first : first + width]
+            else:
+                width = 512
+                codes, scales = w_codes[u][:], w_scales[u][:]
+            nc.vector.quantize_mx(out=codes.bitcast(FP8X4), scales=scales, in_=grouped[u][:, : width * PACK])
 
-        def gather(table, picked, a=0, b=S):
+        def gather(table, picked, a, b):
             nc.vector.tensor_copy(picked[:, a:b], table[:].indirect(offsets[:, a // 16 : b // 16]))
 
-        for s in range(PASSES):
-            for q, (first, width) in enumerate(X_LOADS[s]):
-                u = ("x", s, q)
-                share = 336 if width == 512 else 96
-                interleave(u, "scalar", 0, share)
-                interleave(u, "vector", share, width)
-                quantise(u)
-                if (s, q) == (1, 0):
-                    gather(x_codes[0], g_codes[0])
-                if (s, q) == (1, 1):
-                    gather(x_scales[0], g_scales[0])
-        gather(x_scales[1], g_scales[1])
-        gather(x_codes[1], g_codes[1], 0, HALF)
-        interleave("w1_0", "scalar", 0, 448)
-        interleave("w1_0", "vector", 448, 512)
-        quantise("w1_0")
-        gather(x_codes[1], g_codes[1], HALF, S)
-        interleave("w1_1", "scalar", 0, 448)
-        interleave("w1_1", "vector", 448, 512)
-        quantise("w1_1")
-
-        def product(acc, name, t, s, cols, start, stop):
-            codes, scales = w_codes[name]
-            rows = slice(t * P, (t + 1) * P)
+        def product(acc, lhs, lhs_scale, s, cols, start, stop):
             nc.tensor.matmul_mx(
                 out=acc,
-                lhsT=codes[:, rows].bitcast(FP8X4),
-                lhsT_scale=scales[:, rows],
+                lhsT=lhs.bitcast(FP8X4),
+                lhsT_scale=lhs_scale,
                 rhs=g_codes[s][:, cols].bitcast(FP8X4),
-                rhs_scale=g_scales[s][:, cols],
+                rhs_scale=g_scales[s][row0[s] :, cols],
                 start=start,
                 stop=stop,
             )
 
-        warm = psum.tile([P, HALF], F32, name="bank")
-        for e in range(4):
-            nc.tensor.matmul_mx(
-                out=warm[:],
-                lhsT=g_codes[1][:, 0:P].bitcast(FP8X4),
-                lhsT_scale=g_scales[1][:, 0:P],
-                rhs=g_codes[1][:, 0:HALF].bitcast(FP8X4),
-                rhs_scale=g_scales[1][:, 0:HALF],
-                start=True,
-                stop=True,
-            )
-        banks = {}
-        gates = []
-        for half in range(2):
-            gates.append(keep.tile([P, PACK, HALF], F32, name=f"gate{half}"))
-            for t in range(PACK):
-                banks[half, t] = psum.tile([P, HALF], F32, name="bank")
-        for s in range(PASSES):
-            for half in range(2):
-                for t in range(PACK):
-                    product(banks[half, t][:], f"w1_{s}", t, s, slice(half * HALF, (half + 1) * HALF), s == 0, s == 1)
-        interleave("w3_0", "scalar", 0, 256)
-        interleave("w3_0", "vector", 256, 512)
-        quantise("w3_0")
-        interleave("w3_1", "scalar", 0, 256)
-        interleave("w3_1", "scalar", 256, 352)
-        interleave("w3_1", "vector", 352, 512)
-        quantise("w3_1")
-        for half in range(2):
-            for t in range(PACK):
-                nc.scalar.activation(gates[half][:, t, :], banks[half, t][:], SIGMOID)
+        def warm_up(s, n):
+            acc = psum.tile([P, HALF], F32, name="bank")
+            for e in range(n):
+                product(acc[:], g_codes[s][:, 0:P], g_scales[s][row0[s] :, 0:P], s, slice(0, HALF), True, True)
 
+        banks = {}
+        gates = [keep.tile([P, PACK, HALF], F32, name=f"gate{half}") for half in range(2)]
+        strips = {}
         h_grouped = keep.tile([P, S * PACK], BF16, name="h_grouped", align_bytes=64)
         h_codes = keep.tile([P, S], U32, name="h_codes", align_bytes=64)
         h_scales = keep.tile([P, S], U8, name="h_scales", align_bytes=64)
-        out_rows = out.rearrange("(b p) n -> p b n", p=P)
 
-        def second(first, width, engines):
-            cols = slice(first, first + width)
-            codes, scales = w_codes["w2"]
-            y = keep.tile([P, N // P, width], F32, name=f"y{first}")
-            per_bank = HALF // width
-            for g in range(N // P // per_bank):
-                acc = psum.tile([P, per_bank, width], F32, name="bank")
-                for e in range(per_bank):
-                    b = per_bank * g + e
-                    rows = slice(b * P, (b + 1) * P)
-                    nc.tensor.matmul_mx(
-                        out=acc[:, e, :],
-                        lhsT=codes[:, rows].bitcast(FP8X4),
-                        lhsT_scale=scales[:, rows],
-                        rhs=h_codes[:, cols].bitcast(FP8X4),
-                        rhs_scale=h_scales[:, cols],
-                        start=True,
-                        stop=True,
-                    )
-                group = y[:, per_bank * g : per_bank * (g + 1), :]
-                if engines[g] == "S":
-                    nc.scalar.copy(group, acc[:])
-                else:
-                    nc.vector.tensor_copy(group, acc[:])
-                nc.sync.dma_start(out=out_rows[:, per_bank * g : per_bank * (g + 1), cols], in_=group)
+        def weights(u, t):
+            return w_codes[u][:, t * P : (t + 1) * P], w_scales[u][:, t * P : (t + 1) * P]
+
+        def first_pass():
+            for half in range(2):
+                for t in range(PACK):
+                    banks[half, t] = psum.tile([P, HALF], F32, name="bank")
+                    product(banks[half, t][:], *weights("w1_0", t), 0, slice(half * HALF, (half + 1) * HALF), True, False)
+
+        def second_pass(half, t):
+            product(banks[half, t][:], *weights("w1_1", t), 1, slice(half * HALF, (half + 1) * HALF), False, True)
+
+        def gate(half, t):
+            nc.scalar.activation(gates[half][:, t, :], banks[half, t][:], SIGMOID)
+
+        def linear(c):
+            strips[c] = psum.tile([P, PACK, STRIP], F32, name="bank")
+            for t in range(PACK):
+                for s in range(PASSES):
+                    product(strips[c][:, t, :], *weights(f"w3_{s}", t), s, slice(c * STRIP, (c + 1) * STRIP), s == 0, s == 1)
 
         def gated(c):
-            acc = strips[c]
             half, first = divmod(c * STRIP, HALF)
             nc.vector.tensor_tensor(
                 out=h_grouped[:, c * STRIP * PACK : (c + 1) * STRIP * PACK].rearrange("p (c i t) -> p c t i", i=4, t=PACK),
-                in0=acc[:].rearrange("p t (c i) -> p c t i", i=4),
+                in0=strips[c][:].rearrange("p t (c i) -> p c t i", i=4),
                 in1=gates[half][:, :, first : first + STRIP].rearrange("p t (c i) -> p c t i", i=4),
                 op=MULT,
             )
@@ -226,26 +157,135 @@ def tile_picked_pick_glu_sigmoid_srt_e_kernel(tc, xT, w1, w3, w2, offs, out):
                 in_=h_grouped[:, c * STRIP * PACK : (c + n) * STRIP * PACK],
             )
 
-        strips = {}
-        for c in range(STRIPS):
-            strips[c] = psum.tile([P, PACK, STRIP], F32, name="bank")
-            for t in range(PACK):
-                for s in range(PASSES):
-                    product(strips[c][:, t, :], f"w3_{s}", t, s, slice(c * STRIP, (c + 1) * STRIP), s == 0, s == 1)
-            gated(c)
-            if c == 2:
-                quantise_h(0, 2)
-                interleave("w2", "vector", 0, 512)
-                quantise("w2")
-            if c == 4:
-                quantise_h(2, 2)
-                second(0, 256, "SS")
-            if c == 6:
-                quantise_h(4, 2)
-                second(256, 256, "SS")
-            if c == 7:
-                second(512, 256, "SS")
-                quantise_h(6, 1)
-                second(768, 128, "S")
-                quantise_h(7, 1)
-                second(896, 128, "V")
+        out_rows = out.rearrange("(b p) n -> p b n", p=P)
+        y_acc = {}
+
+        def output(first, width, g):
+            cols = slice(first, first + width)
+            per_bank = HALF // width
+            y_acc[first, g] = psum.tile([P, per_bank, width], F32, name="bank")
+            for e in range(per_bank):
+                lhs, lhs_scale = weights("w2", per_bank * g + e)
+                nc.tensor.matmul_mx(
+                    out=y_acc[first, g][:, e, :],
+                    lhsT=lhs.bitcast(FP8X4),
+                    lhsT_scale=lhs_scale,
+                    rhs=h_codes[:, cols].bitcast(FP8X4),
+                    rhs_scale=h_scales[:, cols],
+                    start=True,
+                    stop=True,
+                )
+
+        def store(first, width, g, copy):
+            per_bank = HALF // width
+            y = keep.tile([P, per_bank, width], F32, name=f"y{first}_{g}")
+            copy(y[:], y_acc[first, g][:])
+            nc.sync.dma_start(out=out_rows[:, per_bank * g : per_bank * (g + 1), first : first + width], in_=y[:])
+
+        load_x(0, 0, 0, 1024)
+        nc.sync.dma_start(offsets[:], offs)
+        load_x(0, 1, 1024, 1024)
+        load_x(1, 0, 0, 1024)
+        load_x(1, 1, 1024, 512)
+        load_x(1, 2, 1536, 512)
+        load_w("w1_0", 0, 512)
+        load_w("w1_1", 0, 512)
+        load_w("w3_0", 0, 512)
+        load_w("w3_1", 0, 512)
+        load_w("w2", 0, 512)
+        interleave(("x", 0, 0, 0, 512, 0), nc.vector.tensor_copy, 256, 512)
+        interleave(("x", 0, 0, 0, 512, 0), nc.scalar.copy, 0, 256)
+        interleave(("x", 0, 0, 512, 512, 512), nc.vector.tensor_copy, 256, 512)
+        interleave(("x", 0, 0, 512, 512, 512), nc.scalar.copy, 0, 256)
+        quantise(("x", 0, 0, 0, 512, 0))
+        quantise(("x", 0, 0, 512, 512, 512))
+        interleave(("x", 0, 1, 0, 512, 1024), nc.vector.tensor_copy, 256, 512)
+        interleave(("x", 0, 1, 0, 512, 1024), nc.scalar.copy, 0, 256)
+        interleave(("x", 0, 1, 512, 512, 1536), nc.vector.tensor_copy, 256, 512)
+        interleave(("x", 0, 1, 512, 512, 1536), nc.scalar.copy, 0, 256)
+        quantise(("x", 0, 1, 0, 512, 1024))
+        quantise(("x", 0, 1, 512, 512, 1536))
+        gather(x_codes[0], g_codes[0], 0, S)
+        interleave(("x", 1, 0, 0, 512, 0), nc.scalar.copy, 0, 288)
+        interleave(("x", 1, 0, 512, 512, 512), nc.scalar.copy, 0, 288)
+        interleave(("x", 1, 0, 0, 512, 0), nc.vector.tensor_copy, 288, 512)
+        interleave(("x", 1, 0, 512, 512, 512), nc.vector.tensor_copy, 288, 512)
+        quantise(("x", 1, 0, 0, 512, 0))
+        interleave(("x", 1, 1, 0, 512, 1024), nc.scalar.copy, 0, 288)
+        quantise(("x", 1, 0, 512, 512, 512))
+        interleave(("x", 1, 1, 0, 512, 1024), nc.vector.tensor_copy, 288, 512)
+        interleave(("x", 1, 2, 0, 512, 1536), nc.scalar.copy, 0, 256)
+        interleave(("x", 1, 2, 0, 512, 1536), nc.vector.tensor_copy, 256, 512)
+        quantise(("x", 1, 1, 0, 512, 1024))
+        quantise(("x", 1, 2, 0, 512, 1536))
+        interleave("w1_0", nc.scalar.copy, 0, 512)
+        gather(x_scales[1], g_scales[1], 0, S)
+        interleave("w1_1", nc.scalar.copy, 0, 384)
+        gather(x_codes[1], g_codes[1], 0, HALF)
+        warm_up(0, 3)
+        quantise("w1_0")
+        interleave("w1_1", nc.vector.tensor_copy, 384, 512)
+        interleave("w3_0", nc.scalar.copy, 0, 512)
+        first_pass()
+        quantise("w1_1")
+        gather(x_codes[1], g_codes[1], HALF, S)
+        interleave("w3_1", nc.vector.tensor_copy, 64, 512)
+        interleave("w3_1", nc.scalar.copy, 0, 64)
+        second_pass(0, 0)
+        second_pass(0, 1)
+        gate(0, 0)
+        second_pass(0, 2)
+        quantise("w3_0")
+        second_pass(0, 3)
+        second_pass(1, 0)
+        gate(0, 1)
+        second_pass(1, 1)
+        quantise("w3_1")
+        second_pass(1, 2)
+        gate(0, 2)
+        second_pass(1, 3)
+        interleave("w2", nc.vector.tensor_copy, 128, 512)
+        linear(0)
+        gate(0, 3)
+        linear(1)
+        gate(1, 0)
+        linear(2)
+        gated(0)
+        linear(3)
+        gate(1, 1)
+        gated(1)
+        linear(4)
+        gate(1, 2)
+        gated(2)
+        linear(5)
+        gate(1, 3)
+        quantise_h(0, 2)
+        linear(6)
+        gated(3)
+        interleave("w2", nc.scalar.copy, 0, 128)
+        linear(7)
+        gated(4)
+        quantise("w2")
+        quantise_h(2, 2)
+        output(0, 256, 0)
+        gated(5)
+        output(0, 256, 1)
+        store(0, 256, 0, nc.scalar.copy)
+        output(256, 256, 0)
+        output(256, 256, 1)
+        gated(6)
+        store(0, 256, 1, nc.scalar.copy)
+        quantise_h(4, 2)
+        store(256, 256, 0, nc.scalar.copy)
+        quantise_h(6, 1)
+        output(512, 256, 0)
+        gated(7)
+        output(512, 256, 1)
+        store(256, 256, 1, nc.scalar.copy)
+        output(768, 128, 0)
+        quantise_h(7, 1)
+        store(768, 128, 0, nc.vector.tensor_copy)
+        store(512, 256, 0, nc.scalar.copy)
+        output(896, 128, 0)
+        store(896, 128, 0, nc.vector.tensor_copy)
+        store(512, 256, 1, nc.scalar.copy)

@@ -70,18 +70,22 @@ def tile_picked_pick_glu_sigmoid_srt_e_kernel(tc, xT, w1, w3, w2, offs, out):
 
         grouped = {}
 
-        def interleave(u, copy, a, b):
+        def interleave(u, engine, a, b):
             if u not in grouped:
                 grouped[u] = ring.tile([P, 512 * PACK], BF16, name="grouped", align_bytes=64)
             if u[0] == "x":
                 raw = x_raw[u[1], u[2]][:, :, u[3] + a : u[3] + b]
             else:
                 raw = w_raw[u][:, :, a:b]
+            copy = nc.vector.tensor_copy if engine == "V" else nc.scalar.copy
             i = raw.rearrange("p j (c i) -> p c j i", i=4)
             if u[0] == "x" or u == "w2":
                 o = grouped[u][:].rearrange("p (c i j) -> p c j i", i=4, j=PACK)[:, a // 4 : b // 4, :, :]
             else:
                 o = grouped[u][:].rearrange("p (t m j) -> p m j t", t=4, j=PACK)[:, a // 4 : b // 4, :, :]
+                if engine == "V":
+                    copy(o[:, :, :, 0:2], i[:, :, :, 0:2])
+                    o, i = o[:, :, :, 2:4], i[:, :, :, 2:4]
             copy(o, i)
 
         def quantise(u):
@@ -160,9 +164,8 @@ def tile_picked_pick_glu_sigmoid_srt_e_kernel(tc, xT, w1, w3, w2, offs, out):
         out_rows = out.rearrange("(b p) n -> p b n", p=P)
         y_acc = {}
 
-        def output(first, width, g):
+        def output(first, width, per_bank, g):
             cols = slice(first, first + width)
-            per_bank = HALF // width
             y_acc[first, g] = psum.tile([P, per_bank, width], F32, name="bank")
             for e in range(per_bank):
                 lhs, lhs_scale = weights("w2", per_bank * g + e)
@@ -176,8 +179,7 @@ def tile_picked_pick_glu_sigmoid_srt_e_kernel(tc, xT, w1, w3, w2, offs, out):
                     stop=True,
                 )
 
-        def store(first, width, g, copy):
-            per_bank = HALF // width
+        def store(first, width, per_bank, g, copy):
             y = keep.tile([P, per_bank, width], F32, name=f"y{first}_{g}")
             copy(y[:], y_acc[first, g][:])
             nc.sync.dma_start(out=out_rows[:, per_bank * g : per_bank * (g + 1), first : first + width], in_=y[:])
@@ -193,99 +195,102 @@ def tile_picked_pick_glu_sigmoid_srt_e_kernel(tc, xT, w1, w3, w2, offs, out):
         load_w("w3_0", 0, 512)
         load_w("w3_1", 0, 512)
         load_w("w2", 0, 512)
-        interleave(("x", 0, 0, 0, 512, 0), nc.vector.tensor_copy, 256, 512)
-        interleave(("x", 0, 0, 0, 512, 0), nc.scalar.copy, 0, 256)
-        interleave(("x", 0, 0, 512, 512, 512), nc.vector.tensor_copy, 256, 512)
-        interleave(("x", 0, 0, 512, 512, 512), nc.scalar.copy, 0, 256)
+        interleave(("x", 0, 0, 0, 512, 0), "V", 256, 512)
+        interleave(("x", 0, 0, 0, 512, 0), "S", 0, 256)
+        interleave(("x", 0, 0, 512, 512, 512), "V", 256, 512)
+        interleave(("x", 0, 0, 512, 512, 512), "S", 0, 256)
         quantise(("x", 0, 0, 0, 512, 0))
         quantise(("x", 0, 0, 512, 512, 512))
-        interleave(("x", 0, 1, 0, 512, 1024), nc.vector.tensor_copy, 256, 512)
-        interleave(("x", 0, 1, 0, 512, 1024), nc.scalar.copy, 0, 256)
-        interleave(("x", 0, 1, 512, 512, 1536), nc.vector.tensor_copy, 256, 512)
-        interleave(("x", 0, 1, 512, 512, 1536), nc.scalar.copy, 0, 256)
+        interleave(("x", 0, 1, 0, 512, 1024), "V", 256, 512)
+        interleave(("x", 0, 1, 0, 512, 1024), "S", 0, 256)
+        interleave(("x", 0, 1, 512, 512, 1536), "V", 256, 512)
+        interleave(("x", 0, 1, 512, 512, 1536), "S", 0, 256)
         quantise(("x", 0, 1, 0, 512, 1024))
         quantise(("x", 0, 1, 512, 512, 1536))
         gather(x_codes[0], g_codes[0], 0, S)
-        interleave(("x", 1, 0, 0, 512, 0), nc.scalar.copy, 0, 288)
-        interleave(("x", 1, 0, 512, 512, 512), nc.scalar.copy, 0, 288)
-        interleave(("x", 1, 0, 0, 512, 0), nc.vector.tensor_copy, 288, 512)
-        interleave(("x", 1, 0, 512, 512, 512), nc.vector.tensor_copy, 288, 512)
+        interleave(("x", 1, 0, 0, 512, 0), "S", 0, 288)
+        interleave(("x", 1, 0, 512, 512, 512), "S", 0, 288)
+        interleave(("x", 1, 0, 0, 512, 0), "V", 288, 512)
+        interleave(("x", 1, 0, 512, 512, 512), "V", 288, 512)
         quantise(("x", 1, 0, 0, 512, 0))
-        interleave(("x", 1, 1, 0, 512, 1024), nc.scalar.copy, 0, 288)
+        interleave(("x", 1, 1, 0, 512, 1024), "S", 0, 288)
         quantise(("x", 1, 0, 512, 512, 512))
-        interleave(("x", 1, 1, 0, 512, 1024), nc.vector.tensor_copy, 288, 512)
-        interleave(("x", 1, 2, 0, 512, 1536), nc.scalar.copy, 0, 256)
-        interleave(("x", 1, 2, 0, 512, 1536), nc.vector.tensor_copy, 256, 512)
+        interleave(("x", 1, 1, 0, 512, 1024), "V", 288, 512)
+        interleave(("x", 1, 2, 0, 512, 1536), "S", 0, 256)
+        interleave(("x", 1, 2, 0, 512, 1536), "V", 256, 512)
         quantise(("x", 1, 1, 0, 512, 1024))
         quantise(("x", 1, 2, 0, 512, 1536))
-        interleave("w1_0", nc.scalar.copy, 0, 512)
+        interleave("w1_0", "S", 0, 512)
         gather(x_scales[1], g_scales[1], 0, S)
-        interleave("w1_1", nc.scalar.copy, 0, 384)
+        interleave("w1_1", "S", 0, 448)
         gather(x_codes[1], g_codes[1], 0, HALF)
-        warm_up(0, 3)
+        warm_up(0, 2)
         quantise("w1_0")
-        interleave("w1_1", nc.vector.tensor_copy, 384, 512)
-        interleave("w3_0", nc.scalar.copy, 0, 512)
+        interleave("w1_1", "V", 448, 512)
         first_pass()
+        interleave("w3_0", "S", 0, 512)
         quantise("w1_1")
         gather(x_codes[1], g_codes[1], HALF, S)
-        interleave("w3_1", nc.vector.tensor_copy, 64, 512)
-        interleave("w3_1", nc.scalar.copy, 0, 64)
+        interleave("w3_1", "V", 128, 512)
         second_pass(0, 0)
+        interleave("w3_1", "S", 0, 128)
         second_pass(0, 1)
-        gate(0, 0)
         second_pass(0, 2)
         quantise("w3_0")
         second_pass(0, 3)
-        second_pass(1, 0)
         gate(0, 1)
-        second_pass(1, 1)
+        second_pass(1, 0)
         quantise("w3_1")
+        second_pass(1, 1)
         second_pass(1, 2)
         gate(0, 2)
         second_pass(1, 3)
-        interleave("w2", nc.vector.tensor_copy, 128, 512)
-        linear(0)
-        gate(0, 3)
+        interleave("w2", "V", 0, 512)
         linear(1)
-        gate(1, 0)
+        gate(0, 0)
         linear(2)
-        gated(0)
+        gate(0, 3)
+        quantise("w2")
+        linear(0)
+        gate(1, 3)
         linear(3)
-        gate(1, 1)
         gated(1)
-        linear(4)
-        gate(1, 2)
+        gate(1, 1)
+        gated(0)
+        linear(7)
+        gate(1, 0)
         gated(2)
         linear(5)
-        gate(1, 3)
+        gate(1, 2)
         quantise_h(0, 2)
-        linear(6)
+        linear(4)
         gated(3)
-        interleave("w2", nc.scalar.copy, 0, 128)
-        linear(7)
-        gated(4)
-        quantise("w2")
-        quantise_h(2, 2)
-        output(0, 256, 0)
+        output(0, 256, 2, 0)
+        output(0, 256, 2, 1)
         gated(5)
-        output(0, 256, 1)
-        store(0, 256, 0, nc.scalar.copy)
-        output(256, 256, 0)
-        output(256, 256, 1)
-        gated(6)
-        store(0, 256, 1, nc.scalar.copy)
+        store(0, 256, 2, 0, nc.scalar.copy)
+        linear(6)
+        quantise_h(2, 2)
+        store(0, 256, 2, 1, nc.scalar.copy)
+        gated(4)
+        output(256, 256, 2, 0)
+        output(256, 256, 2, 1)
+        store(256, 256, 2, 0, nc.scalar.copy)
         quantise_h(4, 2)
-        store(256, 256, 0, nc.scalar.copy)
-        quantise_h(6, 1)
-        output(512, 256, 0)
         gated(7)
-        output(512, 256, 1)
-        store(256, 256, 1, nc.scalar.copy)
-        output(768, 128, 0)
+        store(256, 256, 2, 1, nc.scalar.copy)
+        output(512, 256, 2, 0)
+        output(512, 256, 2, 1)
         quantise_h(7, 1)
-        store(768, 128, 0, nc.vector.tensor_copy)
-        store(512, 256, 0, nc.scalar.copy)
-        output(896, 128, 0)
-        store(896, 128, 0, nc.vector.tensor_copy)
-        store(512, 256, 1, nc.scalar.copy)
+        store(512, 256, 2, 0, nc.scalar.copy)
+        gated(6)
+        output(896, 128, 2, 0)
+        output(896, 128, 2, 1)
+        store(512, 256, 2, 1, nc.scalar.copy)
+        store(896, 128, 2, 0, nc.vector.tensor_copy)
+        quantise_h(6, 1)
+        store(896, 128, 2, 1, nc.scalar.copy)
+        output(768, 128, 2, 0)
+        output(768, 128, 2, 1)
+        store(768, 128, 2, 0, nc.vector.tensor_copy)
+        store(768, 128, 2, 1, nc.scalar.copy)

@@ -184,12 +184,10 @@ def tile_picked_pick_glu_sigmoid_srt_e_kernel(tc, xT, w1, w3, w2, offs, out):
             copy(y[:], y_acc[first, g][:])
             nc.sync.dma_start(out=out_rows[:, per_bank * g : per_bank * (g + 1), first : first + width], in_=y[:])
 
-        load_x(0, 0, 0, 1024)
+        load_x(0, 0, 0, 2048)
         nc.sync.dma_start(offsets[:], offs)
-        load_x(0, 1, 1024, 1024)
         load_x(1, 0, 0, 1024)
-        load_x(1, 1, 1024, 512)
-        load_x(1, 2, 1536, 512)
+        load_x(1, 1, 1024, 1024)
         load_w("w1_0", 0, 512)
         load_w("w1_1", 0, 512)
         load_w("w3_0", 0, 512)
@@ -199,75 +197,74 @@ def tile_picked_pick_glu_sigmoid_srt_e_kernel(tc, xT, w1, w3, w2, offs, out):
         interleave(("x", 0, 0, 0, 512, 0), "S", 0, 256)
         interleave(("x", 0, 0, 512, 512, 512), "V", 256, 512)
         interleave(("x", 0, 0, 512, 512, 512), "S", 0, 256)
+        interleave(("x", 0, 0, 1024, 512, 1024), "V", 256, 512)
         quantise(("x", 0, 0, 0, 512, 0))
+        interleave(("x", 0, 0, 1024, 512, 1024), "S", 0, 256)
+        interleave(("x", 0, 0, 1536, 512, 1536), "V", 256, 512)
         quantise(("x", 0, 0, 512, 512, 512))
-        interleave(("x", 0, 1, 0, 512, 1024), "V", 256, 512)
-        interleave(("x", 0, 1, 0, 512, 1024), "S", 0, 256)
-        interleave(("x", 0, 1, 512, 512, 1536), "V", 256, 512)
-        interleave(("x", 0, 1, 512, 512, 1536), "S", 0, 256)
-        quantise(("x", 0, 1, 0, 512, 1024))
-        quantise(("x", 0, 1, 512, 512, 1536))
-        gather(x_codes[0], g_codes[0], 0, S)
-        interleave(("x", 1, 0, 0, 512, 0), "S", 0, 288)
-        interleave(("x", 1, 0, 512, 512, 512), "S", 0, 288)
+        interleave(("x", 0, 0, 1536, 512, 1536), "S", 0, 256)
+        quantise(("x", 0, 0, 1024, 512, 1024))
         interleave(("x", 1, 0, 0, 512, 0), "V", 288, 512)
+        interleave(("x", 1, 0, 0, 512, 0), "S", 0, 288)
+        quantise(("x", 0, 0, 1536, 512, 1536))
         interleave(("x", 1, 0, 512, 512, 512), "V", 288, 512)
+        interleave(("x", 1, 0, 512, 512, 512), "S", 0, 288)
+        gather(x_codes[0], g_codes[0], 0, S)
         quantise(("x", 1, 0, 0, 512, 0))
-        interleave(("x", 1, 1, 0, 512, 1024), "S", 0, 288)
         quantise(("x", 1, 0, 512, 512, 512))
+        interleave(("x", 1, 1, 0, 512, 1024), "S", 0, 288)
         interleave(("x", 1, 1, 0, 512, 1024), "V", 288, 512)
-        interleave(("x", 1, 2, 0, 512, 1536), "S", 0, 256)
-        interleave(("x", 1, 2, 0, 512, 1536), "V", 256, 512)
+        interleave(("x", 1, 1, 512, 512, 1536), "V", 128, 512)
+        interleave(("x", 1, 1, 512, 512, 1536), "S", 0, 128)
         quantise(("x", 1, 1, 0, 512, 1024))
-        quantise(("x", 1, 2, 0, 512, 1536))
         interleave("w1_0", "S", 0, 512)
+        quantise(("x", 1, 1, 512, 512, 1536))
         gather(x_scales[1], g_scales[1], 0, S)
-        interleave("w1_1", "S", 0, 448)
-        gather(x_codes[1], g_codes[1], 0, HALF)
-        warm_up(0, 2)
+        interleave("w1_1", "S", 0, 320)
         quantise("w1_0")
-        interleave("w1_1", "V", 448, 512)
+        interleave("w1_1", "V", 320, 512)
         first_pass()
+        gather(x_codes[1], g_codes[1], 0, HALF)
         interleave("w3_0", "S", 0, 512)
         quantise("w1_1")
         gather(x_codes[1], g_codes[1], HALF, S)
-        interleave("w3_1", "V", 128, 512)
         second_pass(0, 0)
+        interleave("w3_1", "V", 128, 512)
         interleave("w3_1", "S", 0, 128)
         second_pass(0, 1)
         second_pass(0, 2)
-        quantise("w3_0")
         second_pass(0, 3)
-        gate(0, 1)
-        second_pass(1, 0)
-        quantise("w3_1")
-        second_pass(1, 1)
-        second_pass(1, 2)
-        gate(0, 2)
-        second_pass(1, 3)
-        interleave("w2", "V", 0, 512)
-        linear(1)
         gate(0, 0)
-        linear(2)
-        gate(0, 3)
-        quantise("w2")
+        second_pass(1, 0)
+        quantise("w3_0")
+        second_pass(1, 1)
+        gate(0, 1)
+        second_pass(1, 2)
+        quantise("w3_1")
+        second_pass(1, 3)
+        gate(0, 2)
+        interleave("w2", "V", 128, 512)
         linear(0)
-        gate(1, 3)
-        linear(3)
-        gated(1)
+        gate(0, 3)
+        linear(1)
         gate(1, 1)
         gated(0)
-        linear(7)
-        gate(1, 0)
+        linear(2)
+        gate(1, 3)
+        gated(1)
+        linear(3)
+        interleave("w2", "S", 0, 128)
         gated(2)
         linear(5)
-        gate(1, 2)
+        gate(1, 0)
         quantise_h(0, 2)
+        quantise("w2")
+        gate(1, 2)
         linear(4)
         gated(3)
         output(0, 256, 2, 0)
-        output(0, 256, 2, 1)
         gated(5)
+        output(0, 256, 2, 1)
         store(0, 256, 2, 0, nc.scalar.copy)
         linear(6)
         quantise_h(2, 2)
@@ -276,21 +273,22 @@ def tile_picked_pick_glu_sigmoid_srt_e_kernel(tc, xT, w1, w3, w2, offs, out):
         output(256, 256, 2, 0)
         output(256, 256, 2, 1)
         store(256, 256, 2, 0, nc.scalar.copy)
+        linear(7)
         quantise_h(4, 2)
-        gated(7)
+        gated(6)
         store(256, 256, 2, 1, nc.scalar.copy)
         output(512, 256, 2, 0)
         output(512, 256, 2, 1)
-        quantise_h(7, 1)
         store(512, 256, 2, 0, nc.scalar.copy)
-        gated(6)
+        quantise_h(6, 1)
+        gated(7)
+        output(768, 128, 2, 0)
+        store(512, 256, 2, 1, nc.scalar.copy)
+        output(768, 128, 2, 1)
+        quantise_h(7, 1)
+        store(768, 128, 2, 0, nc.scalar.copy)
+        store(768, 128, 2, 1, nc.vector.tensor_copy)
         output(896, 128, 2, 0)
         output(896, 128, 2, 1)
-        store(512, 256, 2, 1, nc.scalar.copy)
         store(896, 128, 2, 0, nc.vector.tensor_copy)
-        quantise_h(6, 1)
         store(896, 128, 2, 1, nc.scalar.copy)
-        output(768, 128, 2, 0)
-        output(768, 128, 2, 1)
-        store(768, 128, 2, 0, nc.vector.tensor_copy)
-        store(768, 128, 2, 1, nc.scalar.copy)

from contextlib import ExitStack

import concourse.mybir as mybir

K, T, S, H, N = 1024, 2048, 1024, 512, 512
FLOPS = 2 * S * (2 * K * H + H * N)

F32 = mybir.dt.float32
BF16 = mybir.dt.bfloat16
U32 = mybir.dt.uint32
U16 = mybir.dt.uint16
U8 = mybir.dt.uint8
FP8X4 = mybir.dt.float8_e4m3fn_x4
SIGMOID = mybir.ActivationFunctionType.Sigmoid
MULT = mybir.AluOpType.mult

P = 128
PACK = 4
K_PASS = P * PACK
PASSES = K // K_PASS
HALF = 512
STRIP = 128
STRIPS = S // STRIP
PACKED = True


def tile_picked_pick_glu_sigmoid_srt_e_kernel(tc, xT, w1, w3, w2, offs, out):
    nc = tc.nc

    with ExitStack() as ctx:
        lists = ctx.enter_context(tc.tile_pool(name="lists", bufs=1))
        keep = ctx.enter_context(tc.tile_pool(name="keep", bufs=1))
        ring = ctx.enter_context(tc.tile_pool(name="ring", bufs=5))
        psum = ctx.enter_context(tc.psum_pool(name="psum", bufs=8))

        offsets = lists.tile([P, S // 16], U16, name="offsets")

        x_codes = [keep.tile([P, T], U32, name=f"x_codes{s}", align_bytes=64) for s in range(PASSES)]
        g_codes = [keep.tile([P, S], U32, name=f"g_codes{s}", align_bytes=64) for s in range(PASSES)]
        if PACKED:
            x_plane = keep.tile([P, T], U8, name="x_plane", align_bytes=64)
            g_plane = keep.tile([P, S], U8, name="g_plane", align_bytes=64)
            x_scales = [x_plane, x_plane]
            g_scales = [g_plane, g_plane]
        else:
            x_scales = [keep.tile([P, T], U8, name=f"x_scales{s}", align_bytes=64) for s in range(PASSES)]
            g_scales = [keep.tile([P, S], U8, name=f"g_scales{s}", align_bytes=64) for s in range(PASSES)]
        row0 = (0, 4) if PACKED else (0, 0)

        warm_in = keep.tile([P, 1], F32, name="warm_in")
        warm_out = keep.tile([P, 1], F32, name="warm_out")
        nc.gpsimd.memset(warm_in[:], 0.0)
        nc.scalar.activation(warm_out[:], warm_in[:], SIGMOID)
        for plane in x_scales[:1] if PACKED else x_scales:
            nc.gpsimd.memset(plane[:], 0)

        w_src = {"w1_0": w1[0:K_PASS, :], "w1_1": w1[K_PASS:K, :], "w3_0": w3[0:K_PASS, :], "w3_1": w3[K_PASS:K, :], "w2": w2}
        w_raw = {u: keep.tile([P, PACK, 512], F32, name=f"{u}_raw") for u in w_src}
        w_codes = {u: keep.tile([P, 512], U32, name=f"{u}_codes", align_bytes=64) for u in w_src}
        w_scales = {u: keep.tile([P, 512], U8, name=f"{u}_scales", align_bytes=64) for u in w_src}
        x_raw = {}

        def load_x(s, j, first, width):
            x_raw[s, j] = keep.tile([P, PACK, width], F32, name=f"x_raw{s}_{j}")
            src = xT[s * K_PASS : (s + 1) * K_PASS, first : first + width]
            nc.sync.dma_start(out=x_raw[s, j][:], in_=src.rearrange("(p j) c -> p j c", j=PACK))

        def load_w(u, a, b):
            nc.sync.dma_start(out=w_raw[u][:, :, a:b], in_=w_src[u].rearrange("(p j) c -> p j c", j=PACK)[:, :, a:b])

        grouped = {}

        def interleave(u, engine, a, b):
            if u not in grouped:
                grouped[u] = ring.tile([P, 512 * PACK], BF16, name="grouped", align_bytes=64)
            if u[0] == "x":
                raw = x_raw[u[1], u[2]][:, :, u[3] + a : u[3] + b]
            else:
                raw = w_raw[u][:, :, a:b]
            copy = nc.vector.tensor_copy if engine == "V" else nc.scalar.copy
            i = raw.rearrange("p j (c i) -> p c j i", i=4)
            if u[0] == "x" or u == "w2":
                o = grouped[u][:].rearrange("p (c i j) -> p c j i", i=4, j=PACK)[:, a // 4 : b // 4, :, :]
            else:
                o = grouped[u][:].rearrange("p (t m j) -> p m j t", t=4, j=PACK)[:, a // 4 : b // 4, :, :]
                if engine == "V":
                    copy(o[:, :, :, 0:2], i[:, :, :, 0:2])
                    o, i = o[:, :, :, 2:4], i[:, :, :, 2:4]
            copy(o, i)

        def quantise(u):
            if u[0] == "x":
                s, width, first = u[1], u[4], u[5]
                codes, scales = x_codes[s][:, first : first + width], x_scales[s][row0[s] :, first : first + width]
            else:
                width = 512
                codes, scales = w_codes[u][:], w_scales[u][:]
            nc.vector.quantize_mx(out=codes.bitcast(FP8X4), scales=scales, in_=grouped[u][:, : width * PACK])

        def gather(table, picked, a, b):
            nc.vector.tensor_copy(picked[:, a:b], table[:].indirect(offsets[:, a // 16 : b // 16]))

        def product(acc, lhs, lhs_scale, s, cols, start, stop):
            nc.tensor.matmul_mx(
                out=acc,
                lhsT=lhs.bitcast(FP8X4),
                lhsT_scale=lhs_scale,
                rhs=g_codes[s][:, cols].bitcast(FP8X4),
                rhs_scale=g_scales[s][row0[s] :, cols],
                start=start,
                stop=stop,
            )

        def warm_up(s, n):
            acc = psum.tile([P, HALF], F32, name="bank")
            for e in range(n):
                product(acc[:], g_codes[s][:, 0:P], g_scales[s][row0[s] :, 0:P], s, slice(0, HALF), True, True)

        banks = {}
        gates = [keep.tile([P, PACK, HALF], F32, name=f"gate{half}") for half in range(2)]
        strips = {}
        h_grouped = keep.tile([P, S * PACK], BF16, name="h_grouped", align_bytes=64)
        h_codes = keep.tile([P, S], U32, name="h_codes", align_bytes=64)
        h_scales = keep.tile([P, S], U8, name="h_scales", align_bytes=64)

        def weights(u, t):
            return w_codes[u][:, t * P : (t + 1) * P], w_scales[u][:, t * P : (t + 1) * P]

        def first_pass():
            for half in range(2):
                for t in range(PACK):
                    banks[half, t] = psum.tile([P, HALF], F32, name="bank")
                    product(banks[half, t][:], *weights("w1_0", t), 0, slice(half * HALF, (half + 1) * HALF), True, False)

        def second_pass(half, t):
            product(banks[half, t][:], *weights("w1_1", t), 1, slice(half * HALF, (half + 1) * HALF), False, True)

        def gate(half, t):
            nc.scalar.activation(gates[half][:, t, :], banks[half, t][:], SIGMOID)

        def linear(c):
            strips[c] = psum.tile([P, PACK, STRIP], F32, name="bank")
            for t in range(PACK):
                for s in range(PASSES):
                    product(strips[c][:, t, :], *weights(f"w3_{s}", t), s, slice(c * STRIP, (c + 1) * STRIP), s == 0, s == 1)

        def gated(c):
            half, first = divmod(c * STRIP, HALF)
            nc.vector.tensor_tensor(
                out=h_grouped[:, c * STRIP * PACK : (c + 1) * STRIP * PACK].rearrange("p (c i t) -> p c t i", i=4, t=PACK),
                in0=strips[c][:].rearrange("p t (c i) -> p c t i", i=4),
                in1=gates[half][:, :, first : first + STRIP].rearrange("p t (c i) -> p c t i", i=4),
                op=MULT,
            )

        def quantise_h(c, n):
            cols = slice(c * STRIP, (c + n) * STRIP)
            nc.vector.quantize_mx(
                out=h_codes[:, cols].bitcast(FP8X4),
                scales=h_scales[:, cols],
                in_=h_grouped[:, c * STRIP * PACK : (c + n) * STRIP * PACK],
            )

        out_rows = out.rearrange("(b p) n -> p b n", p=P)
        y_acc = {}

        def output(first, width, per_bank, g):
            cols = slice(first, first + width)
            y_acc[first, g] = psum.tile([P, per_bank, width], F32, name="bank")
            for e in range(per_bank):
                lhs, lhs_scale = weights("w2", per_bank * g + e)
                nc.tensor.matmul_mx(
                    out=y_acc[first, g][:, e, :],
                    lhsT=lhs.bitcast(FP8X4),
                    lhsT_scale=lhs_scale,
                    rhs=h_codes[:, cols].bitcast(FP8X4),
                    rhs_scale=h_scales[:, cols],
                    start=True,
                    stop=True,
                )

        def store(first, width, per_bank, g, copy):
            y = keep.tile([P, per_bank, width], F32, name=f"y{first}_{g}")
            copy(y[:], y_acc[first, g][:])
            nc.sync.dma_start(out=out_rows[:, per_bank * g : per_bank * (g + 1), first : first + width], in_=y[:])

        load_x(0, 0, 0, 2048)
        nc.sync.dma_start(offsets[:], offs)
        load_x(1, 0, 0, 1024)
        load_x(1, 1, 1024, 1024)
        load_w("w1_0", 0, 512)
        load_w("w1_1", 0, 512)
        load_w("w3_0", 0, 512)
        load_w("w3_1", 0, 512)
        load_w("w2", 0, 512)
        interleave(("x", 0, 0, 0, 512, 0), "V", 256, 512)
        interleave(("x", 0, 0, 0, 512, 0), "S", 0, 256)
        interleave(("x", 0, 0, 512, 512, 512), "V", 256, 512)
        interleave(("x", 0, 0, 512, 512, 512), "S", 0, 256)
        interleave(("x", 0, 0, 1024, 512, 1024), "V", 256, 512)
        quantise(("x", 0, 0, 0, 512, 0))
        interleave(("x", 0, 0, 1024, 512, 1024), "S", 0, 256)
        interleave(("x", 0, 0, 1536, 512, 1536), "V", 256, 512)
        quantise(("x", 0, 0, 512, 512, 512))
        interleave(("x", 0, 0, 1536, 512, 1536), "S", 0, 256)
        quantise(("x", 0, 0, 1024, 512, 1024))
        interleave(("x", 1, 0, 0, 512, 0), "V", 288, 512)
        interleave(("x", 1, 0, 0, 512, 0), "S", 0, 288)
        quantise(("x", 0, 0, 1536, 512, 1536))
        interleave(("x", 1, 0, 512, 512, 512), "V", 288, 512)
        interleave(("x", 1, 0, 512, 512, 512), "S", 0, 288)
        gather(x_codes[0], g_codes[0], 0, S)
        quantise(("x", 1, 0, 0, 512, 0))
        quantise(("x", 1, 0, 512, 512, 512))
        interleave(("x", 1, 1, 0, 512, 1024), "S", 0, 288)
        interleave(("x", 1, 1, 0, 512, 1024), "V", 288, 512)
        interleave(("x", 1, 1, 512, 512, 1536), "V", 128, 512)
        interleave(("x", 1, 1, 512, 512, 1536), "S", 0, 128)
        quantise(("x", 1, 1, 0, 512, 1024))
        interleave("w1_0", "S", 0, 512)
        quantise(("x", 1, 1, 512, 512, 1536))
        gather(x_scales[1], g_scales[1], 0, S)
        interleave("w1_1", "S", 0, 320)
        quantise("w1_0")
        interleave("w1_1", "V", 320, 512)
        first_pass()
        gather(x_codes[1], g_codes[1], 0, HALF)
        interleave("w3_0", "S", 0, 512)
        quantise("w1_1")
        gather(x_codes[1], g_codes[1], HALF, S)
        second_pass(0, 0)
        interleave("w3_1", "V", 128, 512)
        interleave("w3_1", "S", 0, 128)
        second_pass(0, 1)
        second_pass(0, 2)
        second_pass(0, 3)
        gate(0, 0)
        second_pass(1, 0)
        quantise("w3_0")
        second_pass(1, 1)
        gate(0, 1)
        second_pass(1, 2)
        quantise("w3_1")
        second_pass(1, 3)
        gate(0, 2)
        interleave("w2", "V", 128, 512)
        linear(0)
        gate(0, 3)
        linear(1)
        gate(1, 1)
        gated(0)
        linear(2)
        gate(1, 3)
        gated(1)
        linear(3)
        interleave("w2", "S", 0, 128)
        gated(2)
        linear(5)
        gate(1, 0)
        quantise_h(0, 2)
        quantise("w2")
        gate(1, 2)
        linear(4)
        gated(3)
        output(0, 256, 2, 0)
        gated(5)
        output(0, 256, 2, 1)
        store(0, 256, 2, 0, nc.scalar.copy)
        linear(6)
        quantise_h(2, 2)
        store(0, 256, 2, 1, nc.scalar.copy)
        gated(4)
        output(256, 256, 2, 0)
        output(256, 256, 2, 1)
        store(256, 256, 2, 0, nc.scalar.copy)
        linear(7)
        quantise_h(4, 2)
        gated(6)
        store(256, 256, 2, 1, nc.scalar.copy)
        output(512, 256, 2, 0)
        output(512, 256, 2, 1)
        store(512, 256, 2, 0, nc.scalar.copy)
        quantise_h(6, 1)
        gated(7)
        output(768, 128, 2, 0)
        store(512, 256, 2, 1, nc.scalar.copy)
        output(768, 128, 2, 1)
        quantise_h(7, 1)
        store(768, 128, 2, 0, nc.scalar.copy)
        store(768, 128, 2, 1, nc.vector.tensor_copy)
        output(896, 128, 2, 0)
        output(896, 128, 2, 1)
        store(896, 128, 2, 0, nc.vector.tensor_copy)
        store(896, 128, 2, 1, nc.scalar.copy)
